import numpy as np
import ml_dtypes


def mxq(x, axis, fmt="e4m3"):
    dtype, down = {"e4m3": (ml_dtypes.float8_e4m3fn, 7), "e5m2": (ml_dtypes.float8_e5m2, 14)}[fmt]
    v = np.moveaxis(np.asarray(x, np.float32).astype(ml_dtypes.bfloat16).astype(np.float64), axis, -1)
    blocks = v.reshape(v.shape[:-1] + (-1, 32))
    amax = np.abs(blocks).max(-1, keepdims=True)
    byte = np.maximum(np.where(amax > 0, np.frexp(amax)[1] - 1 + 127, 0) - down, 1)
    scale = np.exp2(byte - 127.0)
    codes = (blocks / scale).astype(np.float32).astype(dtype).astype(np.float64)
    return np.moveaxis((codes * scale).reshape(v.shape), -1, axis)


WIDE = False


def mx_kscale(k):
    if not WIDE:
        return np.ones(k)
    levels = np.array([10, -10, 5, -5, 0])
    if k % 512:
        return np.exp2(np.random.permutation(np.resize(levels, k // 32))).repeat(32)
    a = np.empty((k // 512, 16))
    for p in range(k // 512):
        a[p, :8] = np.random.permutation(np.resize(levels, 8))
        for g in range(8):
            far = levels[np.abs(levels - a[p, g]) >= 10]
            a[p, g + 8] = far[np.random.randint(len(far))]
    return np.exp2(a.ravel()).repeat(32)


def f64(x):
    return np.asarray(x).astype(np.float64)


def striped(idx):
    return np.tile(idx.reshape(-1, 16).T, (8, 1)).astype(np.uint16)


def unstriped(offs):
    return offs[:16].T.reshape(-1).astype(np.int64)


E2M1 = np.array([0.0, 0.5, 1.0, 1.5, 2.0, 3.0, 4.0, 6.0, -0.0, -0.5, -1.0, -1.5, -2.0, -3.0, -4.0, -6.0])


def pack_weight(w, fmt):
    k, n = w.shape
    w = f64(np.asarray(w, np.float32).astype(ml_dtypes.bfloat16)).reshape(k // 32, 32, n)
    amax = np.abs(w).max(1)
    if fmt == "e4m3":
        byte = np.frexp(amax)[1] - 1 + 127 - 7
    else:
        mant, ex = np.frexp(amax / 6.0)
        byte = np.where(mant > 0.5, ex, ex - 1) + 127
    byte = np.clip(np.where(amax > 0, byte, 1), 1, 254)
    scaled = (w * np.exp2(127.0 - byte)[:, None, :]).reshape(k, n).astype(np.float32)
    by_word = np.ascontiguousarray(scaled.reshape(k // 512, 128, 4, n).transpose(0, 1, 3, 2))
    if fmt == "e4m3":
        words = by_word.astype(ml_dtypes.float8_e4m3fn).view(np.uint8)
    else:
        c = by_word.astype(ml_dtypes.float4_e2m1fn).view(np.uint8) & 0xF
        words = (c[..., 0::2] | (c[..., 1::2] << 4)).reshape(k // 512, 128, 2 * n)
    return np.ascontiguousarray(words), np.ascontiguousarray(byte.astype(np.uint8).reshape(k // 512, 16, n))


def unpack_weight(words, scales, fmt):
    g, _, n = scales.shape
    words = np.ascontiguousarray(words).reshape(g, 128, n, -1)
    if fmt == "e4m3":
        vals = words.view(ml_dtypes.float8_e4m3fn).astype(np.float64)
    else:
        nib = np.empty((g, 128, n, 4), np.uint8)
        nib[..., 0::2] = words & 0xF
        nib[..., 1::2] = words >> 4
        vals = E2M1[nib]
    vals = vals * np.repeat(np.exp2(scales.astype(np.float64) - 127.0), 8, axis=1)[..., None]
    return vals.transpose(0, 1, 3, 2).reshape(g * 512, n)


def gelu(v):
    return 0.5 * v * (1.0 + np.tanh(np.sqrt(2.0 / np.pi) * (v + 0.044715 * v**3)))


def striped8(idx):
    return np.concatenate([v.reshape(-1, 16).T for v in idx]).astype(np.uint16)


def unstriped8(offs):
    return np.stack([offs[16 * g:16 * g + 16].T.reshape(-1) for g in range(8)]).astype(np.int64)


def put_heads(h, wgs, idx8, t2):
    r = np.arange(h.shape[0])
    page = np.zeros((h.shape[0], t2))
    page[r[:, None], idx8[r % 512 // 64]] = wgs[r // 4 % 128] * h
    return page


K, H, N, T, S, T2 = 1536, 1024, 512, 2048, 1024, 2048

def setup_inputs():
    n = np.random.standard_normal
    s = mx_kscale(K)[:, None]
    u = mx_kscale(H)[:, None]
    tab_words, tab_scales = pack_weight(n((K, T)) * s, "e4m3")
    w1_words, w1_scales = pack_weight(n((K, H)) / np.sqrt(K) / s, "e2m1")
    return {
        "tab_words": tab_words, "tab_scales": tab_scales,
        "offs": striped(np.random.permutation(T)[:S]),
        "w1_words": w1_words, "w1_scales": w1_scales,
        "b1": (0.5 * n(H)).astype(np.float32),
        "gain": (np.random.uniform(0.6, 1.6, H) * u[:, 0]).astype(np.float32),
        "wgs": np.repeat(np.random.uniform(0.5, 2.0, (8, S)), 16, axis=0).astype(np.float32),
        "offs2": striped8(np.stack([np.random.permutation(T2)[:S] for _ in range(8)])),
        "load": (0.7 * n((H, T2)) * u).astype(np.float32),
        "w2": (n((H, N)) / np.sqrt(H) / u).astype(np.float32),
    }

def reference(tab_words, tab_scales, offs, w1_words, w1_scales, b1, gain, wgs, offs2, load, w2):
    v = unpack_weight(tab_words, tab_scales, "e4m3")[:, unstriped(offs)]
    w1 = unpack_weight(w1_words, w1_scales, "e2m1")
    e = (w1.T @ v) + f64(b1)[:, None]
    h = np.tanh(e) * f64(gain)[:, None]
    page = put_heads(h, f64(wgs), unstriped8(offs2), T2)
    z = page + f64(load)
    zq = mxq(z, 0, "e4m3")
    w2q = mxq(f64(w2), 0, "e4m3")
    return w2q.T @ zq

@@ -1,0 +1,292 @@
+from contextlib import ExitStack
+
+import concourse.mybir as mybir
+from concourse.masks import make_identity
+
+K, H, N, T, S, T2 = 1536, 1024, 512, 2048, 1024, 2048
+FLOPS = 2 * K * H * S + 2 * H * N * T2
+
+F32 = mybir.dt.float32
+BF16 = mybir.dt.bfloat16
+I32 = mybir.dt.int32
+U32 = mybir.dt.uint32
+U16 = mybir.dt.uint16
+U8 = mybir.dt.uint8
+FP8X4 = mybir.dt.float8_e4m3fn_x4
+FP4X4 = mybir.dt.float4_e2m1fn_x4
+MULT = mybir.AluOpType.mult
+TANH = mybir.ActivationFunctionType.Tanh
+COPY = mybir.ActivationFunctionType.Copy
+
+P = 128
+PACK = 4
+BANK = 512
+K_PASSES = K // (P * PACK)
+H_PASSES = H // (P * PACK)
+ROW_TILES = H // P
+CHUNKS = T2 // BANK
+N_TILES = N // P
+QUADRANT = 32
+SCALE_ROWS = 4
+PACKED_ROWS = K_PASSES * SCALE_ROWS
+PLANE_ROWS = 3 * QUADRANT + SCALE_ROWS
+PAGES = 4
+PICKED_AT = PAGES * T2 * 4
+WEIGHTS_AT = PICKED_AT + K_PASSES * S * 4
+
+
+def tile_list_crossdock_door_load_kernel(tc, tab_words, tab_scales, offs, w1_words, w1_scales, b1, gain, wgs, offs2, load, w2, out):
+    nc = tc.nc
+    with ExitStack() as ctx:
+        lists = ctx.enter_context(tc.tile_pool(name="lists", bufs=1))
+        keep = ctx.enter_context(tc.tile_pool(name="keep", bufs=1))
+        shared = ctx.enter_context(tc.tile_pool(name="shared", bufs=1))
+        ring = ctx.enter_context(tc.tile_pool(name="ring", bufs=3))
+        psum = ctx.enter_context(tc.psum_pool(name="psum", bufs=1))
+
+        def bank(j):
+            return psum.tile([P, BANK], F32, name="bank%d" % j)
+
+        pick = lists.tile([P, S // 16], U16, name="pick")
+        place = lists.tile([P, S // 16], U16, name="place")
+        table = shared.tile([P, K_PASSES * T], U32, name="table", offset=0, align_bytes=64)
+        tab_packed = keep.tile([P, T], U8, name="tab_packed")
+        w1_packed = keep.tile([P, H], U8, name="w1_packed")
+        w1_raw = keep.tile([P, K_PASSES * 2 * H], U8, name="w1_raw")
+        wgs_sb = keep.tile([P, S], F32, name="wgs_sb")
+        bias = keep.tile([P, H_PASSES, PACK], F32, name="bias")
+        gains = keep.tile([P, H_PASSES, PACK], F32, name="gains")
+        ident = keep.tile([P, P], F32, name="ident")
+
+        def load_table(a):
+            nc.sync.dma_start(out=table[:, a * T : (a + 1) * T].bitcast(I32),
+                              in_=tab_words[a].rearrange("p t i -> p (t i)").bitcast(I32))
+
+        def load_scale_rows(queues, packed, scales):
+            words = packed[:].bitcast(I32)
+            nc.vector.memset(words, 0)
+            for q, queue in enumerate(queues):
+                queue.dma_start(out=words[QUADRANT * q : QUADRANT * q + PACKED_ROWS, :],
+                                in_=scales[:, SCALE_ROWS * q : SCALE_ROWS * (q + 1), :].bitcast(I32))
+
+        def unpack_planes(packed, name):
+            planes = [packed]
+            for a in range(1, K_PASSES):
+                plane = keep.tile([P, S], U8, name="%s%d" % (name, a), align_bytes=64)
+                nc.vector.memset(plane[3 * QUADRANT :, :].bitcast(I32), 0)
+                nc.sync.dma_start(out=plane[:PLANE_ROWS, :].bitcast(I32),
+                                    in_=packed[SCALE_ROWS * a : SCALE_ROWS * a + PLANE_ROWS, :].bitcast(I32))
+                planes.append(plane)
+            return planes
+
+        nc.sync.dma_start(pick[:], offs)
+        load_table(0)
+        load_scale_rows([nc.scalar] * 4, tab_packed, tab_scales)
+        load_scale_rows([nc.sync, nc.sync, nc.scalar, nc.scalar], w1_packed, w1_scales)
+        load_table(1)
+        nc.sync.dma_start(out=w1_raw[:].bitcast(I32).rearrange("p (a c) -> p a c", a=K_PASSES),
+                          in_=w1_words.rearrange("a p c -> p a c").bitcast(I32))
+        load_table(2)
+        nc.sync.dma_start(place[:], offs2)
+        nc.sync.dma_start(out=wgs_sb[:], in_=wgs)
+        nc.gpsimd.dma_start(out=gains[:], in_=gain.rearrange("(b p i) -> p b i", b=H_PASSES, i=PACK))
+        nc.gpsimd.dma_start(out=bias[:], in_=b1.rearrange("(b p i) -> p b i", b=H_PASSES, i=PACK))
+        make_identity(nc, ident[:])
+
+        picked = [shared.tile([P, S], U32, name="picked%d" % a, offset=PICKED_AT + a * S * 4) for a in range(K_PASSES)]
+
+        def gather_words(a, lo, hi):
+            nc.vector.tensor_copy(picked[a][:, lo:hi],
+                                  table[:, a * T : (a + 1) * T].indirect(pick[:, lo // 16 : hi // 16]))
+
+        gather_words(0, 0, S)
+        picked_scales = keep.tile([P, S], U8, name="picked_scales", align_bytes=64)
+        nc.vector.tensor_copy(picked_scales[:], tab_packed[:].indirect(pick[:]))
+        tab_planes = unpack_planes(picked_scales, "tab_planes")
+        w1_scales_ordered = keep.tile([P, H], U8, name="w1_scales_ordered", align_bytes=64)
+        nc.vector.tensor_copy(w1_scales_ordered[:].rearrange("p (b i m) -> p b i m", b=H_PASSES, i=PACK),
+                              w1_packed[:].rearrange("p (b m i) -> p b i m", b=H_PASSES, i=PACK))
+        w1_planes = unpack_planes(w1_scales_ordered, "w1_planes")
+        gather_words(1, 0, S)
+        w1_codes = keep.tile([P, K_PASSES * 2 * H], U8, name="w1_codes", align_bytes=64)
+
+        def order_w1_words(b):
+            nc.vector.tensor_copy(
+                w1_codes[:].bitcast(U16).rearrange("p (a b i m) -> p b a i m", b=H_PASSES, i=PACK, m=P)[:, b],
+                w1_raw[:].bitcast(U16).rearrange("p (a b m i) -> p b a i m", b=H_PASSES, i=PACK, m=P)[:, b])
+
+        order_w1_words(0)
+        gather_words(2, 0, BANK)
+        gather_words(2, BANK, S)
+        order_w1_words(1)
+
+        pages = []
+        for j in range(PAGES):
+            page = shared.tile([P, T2], F32, name="page%d" % j, offset=((j + K_PASSES) % PAGES) * T * 4)
+            if j == 0:
+                nc.vector.memset(page[:], 0.0)
+            else:
+                nc.gpsimd.memset(page[:], 0.0)
+            pages.append(page)
+
+        load_rows = load.rearrange("(b p i) t -> b i p t", b=H_PASSES, i=PACK)
+        w2_rows = w2.rearrange("(b p i) n -> b p i n", b=H_PASSES, i=PACK)
+        h, weight, held = {}, {}, {}
+
+        def first_product(r):
+            b, i = divmod(r, PACK)
+            weight[r] = shared.tile([P, S], F32, name="weight%d" % r, offset=WEIGHTS_AT + r * S * 4)
+            nc.scalar.activation(weight[r][:], wgs_sb[:], COPY, scale=gains[:, b, i : i + 1])
+            h[r] = ring.tile([P, S], F32, name="h")
+            for half in range(S // BANK):
+                cols = slice(half * BANK, (half + 1) * BANK)
+                acc = bank(half)
+                for a in range(K_PASSES):
+                    first = a * H + r * P
+                    nc.tensor.matmul_mx(
+                        out=acc[:],
+                        lhsT=w1_codes[:, 2 * first : 2 * (first + P)].bitcast(FP4X4),
+                        lhsT_scale=w1_planes[a][:, r * P : (r + 1) * P],
+                        rhs=picked[a][:, cols].bitcast(FP8X4),
+                        rhs_scale=tab_planes[a][:, cols],
+                        start=(a == 0), stop=(a == K_PASSES - 1))
+                nc.scalar.activation(h[r][:, cols], acc[:], TANH, bias=bias[:, b, i : i + 1])
+
+        def scatter(r, pieces):
+            width = S // pieces
+            for lo in range(0, S, width):
+                nc.vector.tensor_tensor(pages[r % PAGES][:].indirect(place[:, lo // 16 : (lo + width) // 16]),
+                                        h[r][:, lo : lo + width], weight[r][:, lo : lo + width], MULT)
+
+        def load_held(r):
+            held[r] = ring.tile([P, T2], F32, name="rows", bufs=5)
+            nc.sync.dma_start(out=held[r][:], in_=load_rows[r // PACK, r % PACK])
+
+        def turn(acc, region, src, block, start, stop):
+            nc.tensor.matmul(acc[:, region * P : (region + 1) * P], lhsT=src[:, block * P : (block + 1) * P],
+                             rhs=ident[:], start=start, stop=stop, is_transpose=True)
+
+        def open_sum(pair, j, bank_no):
+            acc = bank(bank_no)
+            for c in range(2):
+                for e in range(2):
+                    turn(acc, 2 * c + e, held[2 * pair + e], 2 * j + c, c + e == 0, False)
+            for c in range(2):
+                turn(acc, 2 * c, pages[(2 * pair) % PAGES], 2 * j + c, False, False)
+            return acc
+
+        turned = {}
+
+        def copy_on(use_vector, dst, src):
+            if use_vector:
+                nc.vector.tensor_copy(dst, src)
+            else:
+                nc.scalar.copy(dst, src)
+
+        def close_sum(pair, j, acc, use_vector):
+            for c in range(2):
+                turn(acc, 2 * c + 1, pages[(2 * pair + 1) % PAGES], 2 * j + c, False, c == 1)
+            q, half = divmod(j, 2)
+            if half == 0:
+                turned[pair, q] = ring.tile([P, 2 * BANK], BF16, name="turned", bufs=12)
+            copy_on(use_vector,
+                    turned[pair, q][:, half * BANK : (half + 1) * BANK].rearrange("t (c p e) -> t c p e", c=2, e=2),
+                    acc[:].rearrange("t (c e p) -> t c p e", c=2, e=2))
+
+        z_grouped, z_codes, z_scales = {}, {}, {}
+
+        def turn_back(b, q, bank_nos, share):
+            grouped = z_grouped[b, q] = ring.tile([P, PACK * BANK], BF16, name="grouped", bufs=6, align_bytes=64)
+            for half in range(2):
+                acc = bank(bank_nos[half])
+                for u in range(2):
+                    words = turned[2 * b + u, q][:].bitcast(F32)
+                    for c in range(2):
+                        turn(acc, 2 * u + c, words, 2 * half + c, True, True)
+                copy_on(share and half == 1,
+                        grouped[:].bitcast(F32)[:, half * BANK : (half + 1) * BANK].rearrange("p (t u) -> p t u", u=2),
+                        acc[:].rearrange("p (u t) -> p t u", u=2))
+
+        def quantize_z(b, q):
+            z_codes[b, q] = keep.tile([P, BANK], U32, name="z_codes%d%d" % (b, q), align_bytes=64)
+            z_scales[b, q] = shared.tile([P, BANK], U8, name="z_scales%d%d" % (b, q),
+                                         offset=WEIGHTS_AT + (ROW_TILES - 1) * S * 4 + (b * CHUNKS + q) * BANK)
+            nc.vector.quantize_mx(out=z_codes[b, q][:].bitcast(FP8X4), scales=z_scales[b, q][:], in_=z_grouped[b, q][:])
+
+        w2_raw, w2_grouped, w2_codes, w2_scales = {}, {}, {}, {}
+
+        def load_w2(b):
+            w2_raw[b] = ring.tile([P, PACK * N], F32, name="rows", bufs=5)
+            nc.sync.dma_start(out=w2_raw[b][:].rearrange("p (i n) -> p i n", i=PACK), in_=w2_rows[b])
+
+        def round_w2(b):
+            w2_grouped[b] = ring.tile([P, PACK * N], BF16, name="grouped", bufs=6, align_bytes=64)
+            nc.scalar.copy(w2_grouped[b][:].rearrange("p (c n i) -> p c i n", i=PACK, n=4),
+                           w2_raw[b][:].rearrange("p (i c n) -> p c i n", i=PACK, n=4))
+
+        def quantize_w2(b):
+            w2_codes[b] = keep.tile([P, N], U32, name="w2_codes%d" % b, align_bytes=64)
+            w2_scales[b] = shared.tile([P, N], U8, name="w2_scales%d" % b, offset=WEIGHTS_AT + PACK * S * 4 + b * N)
+            nc.vector.quantize_mx(out=w2_codes[b][:].bitcast(FP8X4), scales=w2_scales[b][:], in_=w2_grouped[b][:])
+
+        def second_product(q, bank_nos):
+            accs = [bank(no) for no in bank_nos]
+            order = [(b, n) for n in range(N_TILES) for b in range(H_PASSES)]
+            for b, n in sorted(order) if q == 0 else order:
+                cols = slice(n * P, (n + 1) * P)
+                nc.tensor.matmul_mx(
+                    out=accs[n][:],
+                    lhsT=w2_codes[b][:, cols].bitcast(FP8X4), lhsT_scale=w2_scales[b][:, cols],
+                    rhs=z_codes[b, q][:].bitcast(FP8X4), rhs_scale=z_scales[b, q][:],
+                    start=(b == 0), stop=(b == H_PASSES - 1))
+            for n in range(N_TILES):
+                result = shared.tile([P, BANK], F32, name="result", bufs=6, offset=PICKED_AT)
+                copy_on(n == 1 or q + n == 6, result[:], accs[n][:])
+                nc.sync.dma_start(out=out[n * P : (n + 1) * P, q * BANK : (q + 1) * BANK], in_=result[:])
+
+        load_held(0)
+        load_held(1)
+        for b in range(H_PASSES):
+            load_w2(b)
+        first_product(0)
+        first_product(1)
+        last_pair = ROW_TILES // 2 - 1
+        sum_banks = [2, 3, 4, 5, 0, 1, 6, 7]
+        opened = []
+        for r in range(ROW_TILES):
+            pair = r // 2
+            scatter(r, 2 if r == 0 else 1)
+            if r + 2 < ROW_TILES:
+                load_held(r + 2)
+                first_product(r + 2)
+            if r < H_PASSES:
+                round_w2(r)
+            if r == PACK:
+                for b in range(H_PASSES):
+                    quantize_w2(b)
+                for q in range(CHUNKS):
+                    turn_back(0, q, [6, 7], False)
+            if r % 2 == 0:
+                early = sum_banks if pair == last_pair else sum_banks[:4]
+                opened = [open_sum(pair, j, no) for j, no in enumerate(early)]
+            else:
+                if pair == last_pair:
+                    quantize_z(0, 0)
+                for j in range(2 * CHUNKS):
+                    acc = opened[j] if j < len(opened) else open_sum(pair, j, sum_banks[j])
+                    close_sum(pair, j, acc, pair == last_pair and j % 2 == 1)
+
+        def finish_z(q, bank_nos):
+            turn_back(1, q, bank_nos, True)
+            quantize_z(1, q)
+            if q + 1 < CHUNKS:
+                quantize_z(0, q + 1)
+
+        finish_z(0, [2, 3])
+        finish_z(1, [4, 5])
+        second_product(0, [0, 1, 6, 7])
+        finish_z(2, [2, 3])
+        second_product(1, [4, 5, 0, 1])
+        finish_z(3, [6, 7])
+        second_product(2, [2, 3, 4, 5])
+        second_product(3, [0, 1, 6, 7])

@@ -1,7 +1,6 @@
 from contextlib import ExitStack
 
 import concourse.mybir as mybir
-from concourse.masks import make_identity
 
 K, H, N, T, S, T2 = 1536, 1024, 512, 2048, 1024, 2048
 FLOPS = 2 * K * H * S + 2 * H * N * T2
@@ -15,6 +14,7 @@ U8 = mybir.dt.uint8
 FP8X4 = mybir.dt.float8_e4m3fn_x4
 FP4X4 = mybir.dt.float4_e2m1fn_x4
 MULT = mybir.AluOpType.mult
+ADD = mybir.AluOpType.add
 TANH = mybir.ActivationFunctionType.Tanh
 COPY = mybir.ActivationFunctionType.Copy
 
@@ -30,9 +30,12 @@ QUADRANT = 32
 SCALE_ROWS = 4
 PACKED_ROWS = K_PASSES * SCALE_ROWS
 PLANE_ROWS = 3 * QUADRANT + SCALE_ROWS
-PAGES = 4
-PICKED_AT = PAGES * T2 * 4
-WEIGHTS_AT = PICKED_AT + K_PASSES * S * 4
+PAGES = 3
+H_SLOTS = 4
+PICKED_AT = K_PASSES * T * 4
+ROWS_AT = PICKED_AT + K_PASSES * S * 4
+H_AT = ROWS_AT + ROW_TILES * T2 * 4
+PLANES_AT = H_AT + H_SLOTS * S * 4
 
 
 def tile_list_crossdock_door_load_kernel(tc, tab_words, tab_scales, offs, w1_words, w1_scales, b1, gain, wgs, offs2, load, w2, out):
@@ -49,17 +52,16 @@ def tile_list_crossdock_door_load_kernel(tc, tab_words, tab_scales, offs, w1_wor
 
         pick = lists.tile([P, S // 16], U16, name="pick")
         place = lists.tile([P, S // 16], U16, name="place")
-        table = shared.tile([P, K_PASSES * T], U32, name="table", offset=0, align_bytes=64)
+        table = [shared.tile([P, T], U32, name="table%d" % a, offset=a * T * 4, align_bytes=64) for a in range(K_PASSES)]
         tab_packed = keep.tile([P, T], U8, name="tab_packed")
         w1_packed = keep.tile([P, H], U8, name="w1_packed")
         w1_raw = keep.tile([P, K_PASSES * 2 * H], U8, name="w1_raw")
         wgs_sb = keep.tile([P, S], F32, name="wgs_sb")
         bias = keep.tile([P, H_PASSES, PACK], F32, name="bias")
         gains = keep.tile([P, H_PASSES, PACK], F32, name="gains")
-        ident = keep.tile([P, P], F32, name="ident")
 
         def load_table(a):
-            nc.sync.dma_start(out=table[:, a * T : (a + 1) * T].bitcast(I32),
+            nc.sync.dma_start(out=table[a][:].bitcast(I32),
                               in_=tab_words[a].rearrange("p t i -> p (t i)").bitcast(I32))
 
         def load_scale_rows(queues, packed, scales):
@@ -82,7 +84,7 @@ def tile_list_crossdock_door_load_kernel(tc, tab_words, tab_scales, offs, w1_wor
         nc.sync.dma_start(pick[:], offs)
         load_table(0)
         load_scale_rows([nc.scalar] * 4, tab_packed, tab_scales)
-        load_scale_rows([nc.sync, nc.sync, nc.scalar, nc.scalar], w1_packed, w1_scales)
+        load_scale_rows([nc.sync] * 4, w1_packed, w1_scales)
         load_table(1)
         nc.sync.dma_start(out=w1_raw[:].bitcast(I32).rearrange("p (a c) -> p a c", a=K_PASSES),
                           in_=w1_words.rearrange("a p c -> p a c").bitcast(I32))
@@ -91,13 +93,12 @@ def tile_list_crossdock_door_load_kernel(tc, tab_words, tab_scales, offs, w1_wor
         nc.sync.dma_start(out=wgs_sb[:], in_=wgs)
         nc.gpsimd.dma_start(out=gains[:], in_=gain.rearrange("(b p i) -> p b i", b=H_PASSES, i=PACK))
         nc.gpsimd.dma_start(out=bias[:], in_=b1.rearrange("(b p i) -> p b i", b=H_PASSES, i=PACK))
-        make_identity(nc, ident[:])
 
         picked = [shared.tile([P, S], U32, name="picked%d" % a, offset=PICKED_AT + a * S * 4) for a in range(K_PASSES)]
 
         def gather_words(a, lo, hi):
             nc.vector.tensor_copy(picked[a][:, lo:hi],
-                                  table[:, a * T : (a + 1) * T].indirect(pick[:, lo // 16 : hi // 16]))
+                                  table[a][:].indirect(pick[:, lo // 16 : hi // 16]))
 
         gather_words(0, 0, S)
         picked_scales = keep.tile([P, S], U8, name="picked_scales", align_bytes=64)
@@ -108,74 +109,66 @@ def tile_list_crossdock_door_load_kernel(tc, tab_words, tab_scales, offs, w1_wor
                               w1_packed[:].rearrange("p (b m i) -> p b i m", b=H_PASSES, i=PACK))
         w1_planes = unpack_planes(w1_scales_ordered, "w1_planes")
         gather_words(1, 0, S)
-        w1_codes = keep.tile([P, K_PASSES * 2 * H], U8, name="w1_codes", align_bytes=64)
+        w1_codes = [keep.tile([P, K_PASSES * H], U8, name="w1_codes0", align_bytes=64),
+                    shared.tile([P, K_PASSES * H], U8, name="w1_codes1", offset=(K_PASSES - 1) * T * 4)]
 
         def order_w1_words(b):
             nc.vector.tensor_copy(
-                w1_codes[:].bitcast(U16).rearrange("p (a b i m) -> p b a i m", b=H_PASSES, i=PACK, m=P)[:, b],
-                w1_raw[:].bitcast(U16).rearrange("p (a b m i) -> p b a i m", b=H_PASSES, i=PACK, m=P)[:, b])
+                w1_codes[b][:].bitcast(U16).rearrange("p (a i m) -> p i a m", i=PACK, m=P),
+                w1_raw[:].bitcast(U16).rearrange("p (a b m i) -> p b i a m", b=H_PASSES, i=PACK, m=P)[:, b])
 
         order_w1_words(0)
         gather_words(2, 0, BANK)
         gather_words(2, BANK, S)
         order_w1_words(1)
 
-        pages = []
-        for j in range(PAGES):
-            page = shared.tile([P, T2], F32, name="page%d" % j, offset=((j + K_PASSES) % PAGES) * T * 4)
-            if j == 0:
-                nc.vector.memset(page[:], 0.0)
-            else:
-                nc.gpsimd.memset(page[:], 0.0)
-            pages.append(page)
+        pages = [keep.tile([P, T2], F32, name="page%d" % j) for j in range(PAGES - 1)]
+        pages.append(shared.tile([P, T2], F32, name="last_page", offset=0))
+        for page in pages:
+            nc.gpsimd.memset(page[:], 0.0)
+        z_planes = [keep.tile([P, PACK * T2], BF16, name="z_planes0"),
+                    shared.tile([P, PACK * T2], BF16, name="z_planes1", offset=PLANES_AT)]
 
         load_rows = load.rearrange("(b p i) t -> b i p t", b=H_PASSES, i=PACK)
         w2_rows = w2.rearrange("(b p i) n -> b p i n", b=H_PASSES, i=PACK)
         h, weight, held = {}, {}, {}
 
+        def pieces(r):
+            return [(0, 256), (256, 512), (512, S)] if r == 0 else [(0, S)]
+
         def first_product(r):
             b, i = divmod(r, PACK)
-            weight[r] = shared.tile([P, S], F32, name="weight%d" % r, offset=WEIGHTS_AT + r * S * 4)
+            weight[r] = shared.tile([P, S], F32, name="weight%d" % r, offset=ROWS_AT + (r - 1) % ROW_TILES * T2 * 4)
             nc.scalar.activation(weight[r][:], wgs_sb[:], COPY, scale=gains[:, b, i : i + 1])
-            h[r] = ring.tile([P, S], F32, name="h")
+            h[r] = shared.tile([P, S], F32, name="h%d" % r, offset=H_AT + r % H_SLOTS * S * 4)
             for half in range(S // BANK):
                 cols = slice(half * BANK, (half + 1) * BANK)
                 acc = bank(half)
                 for a in range(K_PASSES):
-                    first = a * H + r * P
+                    first = (a * PACK + i) * P
                     nc.tensor.matmul_mx(
                         out=acc[:],
-                        lhsT=w1_codes[:, 2 * first : 2 * (first + P)].bitcast(FP4X4),
+                        lhsT=w1_codes[b][:, 2 * first : 2 * (first + P)].bitcast(FP4X4),
                         lhsT_scale=w1_planes[a][:, r * P : (r + 1) * P],
                         rhs=picked[a][:, cols].bitcast(FP8X4),
                         rhs_scale=tab_planes[a][:, cols],
                         start=(a == 0), stop=(a == K_PASSES - 1))
                 nc.scalar.activation(h[r][:, cols], acc[:], TANH, bias=bias[:, b, i : i + 1])
+            for lo, hi in pieces(r):
+                nc.gpsimd.tensor_tensor(h[r][:, lo:hi], h[r][:, lo:hi], weight[r][:, lo:hi], MULT)
 
-        def scatter(r, pieces):
-            width = S // pieces
-            for lo in range(0, S, width):
-                nc.vector.tensor_tensor(pages[r % PAGES][:].indirect(place[:, lo // 16 : (lo + width) // 16]),
-                                        h[r][:, lo : lo + width], weight[r][:, lo : lo + width], MULT)
+        def scatter(r):
+            for lo, hi in pieces(r):
+                nc.vector.tensor_copy(pages[r % PAGES][:].indirect(place[:, lo // 16 : hi // 16]), h[r][:, lo:hi])
 
         def load_held(r):
-            held[r] = ring.tile([P, T2], F32, name="rows", bufs=5)
+            held[r] = shared.tile([P, T2], F32, name="held%d" % r, offset=ROWS_AT + r * T2 * 4)
             nc.sync.dma_start(out=held[r][:], in_=load_rows[r // PACK, r % PACK])
 
-        def turn(acc, region, src, block, start, stop):
-            nc.tensor.matmul(acc[:, region * P : (region + 1) * P], lhsT=src[:, block * P : (block + 1) * P],
-                             rhs=ident[:], start=start, stop=stop, is_transpose=True)
-
-        def open_sum(pair, j, bank_no):
-            acc = bank(bank_no)
-            for c in range(2):
-                for e in range(2):
-                    turn(acc, 2 * c + e, held[2 * pair + e], 2 * j + c, c + e == 0, False)
-            for c in range(2):
-                turn(acc, 2 * c, pages[(2 * pair) % PAGES], 2 * j + c, False, False)
-            return acc
-
-        turned = {}
+        def add_load(engine, r, lo, hi):
+            b, i = divmod(r, PACK)
+            engine.tensor_tensor(z_planes[b][:, i * T2 + lo : i * T2 + hi], pages[r % PAGES][:, lo:hi],
+                                 held[r][:, lo:hi], ADD)
 
         def copy_on(use_vector, dst, src):
             if use_vector:
@@ -183,110 +176,87 @@ def tile_list_crossdock_door_load_kernel(tc, tab_words, tab_scales, offs, w1_wor
             else:
                 nc.scalar.copy(dst, src)
 
-        def close_sum(pair, j, acc, use_vector):
-            for c in range(2):
-                turn(acc, 2 * c + 1, pages[(2 * pair + 1) % PAGES], 2 * j + c, False, c == 1)
-            q, half = divmod(j, 2)
-            if half == 0:
-                turned[pair, q] = ring.tile([P, 2 * BANK], BF16, name="turned", bufs=12)
-            copy_on(use_vector,
-                    turned[pair, q][:, half * BANK : (half + 1) * BANK].rearrange("t (c p e) -> t c p e", c=2, e=2),
-                    acc[:].rearrange("t (c e p) -> t c p e", c=2, e=2))
-
         z_grouped, z_codes, z_scales = {}, {}, {}
 
-        def turn_back(b, q, bank_nos, share):
-            grouped = z_grouped[b, q] = ring.tile([P, PACK * BANK], BF16, name="grouped", bufs=6, align_bytes=64)
-            for half in range(2):
-                acc = bank(bank_nos[half])
-                for u in range(2):
-                    words = turned[2 * b + u, q][:].bitcast(F32)
-                    for c in range(2):
-                        turn(acc, 2 * u + c, words, 2 * half + c, True, True)
-                copy_on(share and half == 1,
-                        grouped[:].bitcast(F32)[:, half * BANK : (half + 1) * BANK].rearrange("p (t u) -> p t u", u=2),
-                        acc[:].rearrange("p (u t) -> p t u", u=2))
+        def interleave(b, q, vector_cols):
+            z_grouped[b, q] = ring.tile([P, PACK * BANK], BF16, name="grouped", bufs=6, align_bytes=64)
+            planes = z_planes[b][:].rearrange("p (i t) -> p i t", i=PACK)
+            for use_vector, lo, hi in ((False, vector_cols, BANK), (True, 0, vector_cols)):
+                if lo < hi:
+                    copy_on(use_vector,
+                            z_grouped[b, q][:, PACK * lo : PACK * hi].rearrange("p (c t i) -> p c i t", i=PACK, t=4),
+                            planes[:, :, q * BANK + lo : q * BANK + hi].rearrange("p i (c t) -> p c i t", t=4))
 
         def quantize_z(b, q):
             z_codes[b, q] = keep.tile([P, BANK], U32, name="z_codes%d%d" % (b, q), align_bytes=64)
             z_scales[b, q] = shared.tile([P, BANK], U8, name="z_scales%d%d" % (b, q),
-                                         offset=WEIGHTS_AT + (ROW_TILES - 1) * S * 4 + (b * CHUNKS + q) * BANK)
+                                         offset=H_AT + (ROW_TILES - 1) % H_SLOTS * S * 4 + (b * CHUNKS + q) * BANK)
             nc.vector.quantize_mx(out=z_codes[b, q][:].bitcast(FP8X4), scales=z_scales[b, q][:], in_=z_grouped[b, q][:])
 
-        w2_raw, w2_grouped, w2_codes, w2_scales = {}, {}, {}, {}
+        w2_raw = {}
 
         def load_w2(b):
-            w2_raw[b] = ring.tile([P, PACK * N], F32, name="rows", bufs=5)
+            w2_raw[b] = shared.tile([P, PACK * N], F32, name="w2_raw%d" % b, offset=PLANES_AT + b * PACK * N * 4)
             nc.sync.dma_start(out=w2_raw[b][:].rearrange("p (i n) -> p i n", i=PACK), in_=w2_rows[b])
 
         def round_w2(b):
-            w2_grouped[b] = ring.tile([P, PACK * N], BF16, name="grouped", bufs=6, align_bytes=64)
-            nc.scalar.copy(w2_grouped[b][:].rearrange("p (c n i) -> p c i n", i=PACK, n=4),
+            nc.scalar.copy(w2_grouped[:, b * PACK * N : (b + 1) * PACK * N].rearrange("p (c n i) -> p c i n", i=PACK, n=4),
                            w2_raw[b][:].rearrange("p (i c n) -> p c i n", i=PACK, n=4))
-
-        def quantize_w2(b):
-            w2_codes[b] = keep.tile([P, N], U32, name="w2_codes%d" % b, align_bytes=64)
-            w2_scales[b] = shared.tile([P, N], U8, name="w2_scales%d" % b, offset=WEIGHTS_AT + PACK * S * 4 + b * N)
-            nc.vector.quantize_mx(out=w2_codes[b][:].bitcast(FP8X4), scales=w2_scales[b][:], in_=w2_grouped[b][:])
 
         def second_product(q, bank_nos):
             accs = [bank(no) for no in bank_nos]
-            order = [(b, n) for n in range(N_TILES) for b in range(H_PASSES)]
-            for b, n in sorted(order) if q == 0 else order:
-                cols = slice(n * P, (n + 1) * P)
+            for b, n in [(b, n) for b in range(H_PASSES) for n in range(N_TILES)]:
+                cols = slice(b * N + n * P, b * N + (n + 1) * P)
                 nc.tensor.matmul_mx(
                     out=accs[n][:],
-                    lhsT=w2_codes[b][:, cols].bitcast(FP8X4), lhsT_scale=w2_scales[b][:, cols],
+                    lhsT=w2_codes[:, cols].bitcast(FP8X4), lhsT_scale=w2_scales[:, cols],
                     rhs=z_codes[b, q][:].bitcast(FP8X4), rhs_scale=z_scales[b, q][:],
                     start=(b == 0), stop=(b == H_PASSES - 1))
             for n in range(N_TILES):
                 result = shared.tile([P, BANK], F32, name="result", bufs=6, offset=PICKED_AT)
-                copy_on(n == 1 or q + n == 6, result[:], accs[n][:])
+                copy_on(q * N_TILES + n in (11, 13, 15), result[:], accs[n][:])
                 nc.sync.dma_start(out=out[n * P : (n + 1) * P, q * BANK : (q + 1) * BANK], in_=result[:])
 
-        load_held(0)
-        load_held(1)
         for b in range(H_PASSES):
             load_w2(b)
         first_product(0)
         first_product(1)
-        last_pair = ROW_TILES // 2 - 1
-        sum_banks = [2, 3, 4, 5, 0, 1, 6, 7]
-        opened = []
+        load_held(0)
+        w2_grouped = shared.tile([P, H_PASSES * PACK * N], BF16, name="w2_grouped", offset=T * 4)
+        w2_codes = keep.tile([P, H_PASSES * N], U32, name="w2_codes", align_bytes=64)
+        last = ROW_TILES - 1
         for r in range(ROW_TILES):
-            pair = r // 2
-            scatter(r, 2 if r == 0 else 1)
+            scatter(r)
             if r + 2 < ROW_TILES:
-                load_held(r + 2)
                 first_product(r + 2)
+            if r < last:
+                load_held(r + 1)
+                add_load(nc.gpsimd, r, 0, T2)
             if r < H_PASSES:
                 round_w2(r)
-            if r == PACK:
-                for b in range(H_PASSES):
-                    quantize_w2(b)
+            if r == last - 1:
+                w2_scales = shared.tile([P, H_PASSES * N], U8, name="w2_scales", offset=H_AT + r % H_SLOTS * S * 4)
+                nc.vector.quantize_mx(out=w2_codes[:].bitcast(FP8X4), scales=w2_scales[:], in_=w2_grouped[:])
+            if r == PACK + 1:
                 for q in range(CHUNKS):
-                    turn_back(0, q, [6, 7], False)
-            if r % 2 == 0:
-                early = sum_banks if pair == last_pair else sum_banks[:4]
-                opened = [open_sum(pair, j, no) for j, no in enumerate(early)]
-            else:
-                if pair == last_pair:
-                    quantize_z(0, 0)
-                for j in range(2 * CHUNKS):
-                    acc = opened[j] if j < len(opened) else open_sum(pair, j, sum_banks[j])
-                    close_sum(pair, j, acc, pair == last_pair and j % 2 == 1)
+                    interleave(0, q, 0)
 
-        def finish_z(q, bank_nos):
-            turn_back(1, q, bank_nos, True)
-            quantize_z(1, q)
-            if q + 1 < CHUNKS:
-                quantize_z(0, q + 1)
+        def add_last(q):
+            add_load(nc.vector, last, q * BANK, (q + 1) * BANK)
 
-        finish_z(0, [2, 3])
-        finish_z(1, [4, 5])
-        second_product(0, [0, 1, 6, 7])
-        finish_z(2, [2, 3])
-        second_product(1, [4, 5, 0, 1])
-        finish_z(3, [6, 7])
-        second_product(2, [2, 3, 4, 5])
-        second_product(3, [0, 1, 6, 7])
+        add_last(0)
+        add_last(1)
+        interleave(1, 0, BANK // 2)
+        quantize_z(0, 0)
+        quantize_z(1, 0)
+        interleave(1, 1, 0)
+        add_last(2)
+        add_last(3)
+        quantize_z(0, 1)
+        quantize_z(1, 1)
+        for q in range(CHUNKS):
+            if q + 2 < CHUNKS:
+                interleave(1, q + 2, BANK)
+                quantize_z(0, q + 2)
+                quantize_z(1, q + 2)
+            second_product(q, [(q % 2) * N_TILES + n for n in range(N_TILES)])

@@ -1,6 +1,7 @@
 from contextlib import ExitStack
 
 import concourse.mybir as mybir
+from concourse.masks import make_identity
 
 K, H, N, T, S, T2 = 1536, 1024, 512, 2048, 1024, 2048
 FLOPS = 2 * K * H * S + 2 * H * N * T2
@@ -32,6 +33,9 @@ PACKED_ROWS = K_PASSES * SCALE_ROWS
 PLANE_ROWS = 3 * QUADRANT + SCALE_ROWS
 PAGES = 3
 H_SLOTS = 4
+DIRECT_CHUNKS = 2
+DIRECT = DIRECT_CHUNKS * BANK
+SUM_BANKS = (4, 5, 6, 7)
 PICKED_AT = K_PASSES * T * 4
 ROWS_AT = PICKED_AT + K_PASSES * S * 4
 H_AT = ROWS_AT + ROW_TILES * T2 * 4
@@ -89,10 +93,11 @@ def tile_list_crossdock_door_load_kernel(tc, tab_words, tab_scales, offs, w1_wor
         nc.sync.dma_start(out=w1_raw[:].bitcast(I32).rearrange("p (a c) -> p a c", a=K_PASSES),
                           in_=w1_words.rearrange("a p c -> p a c").bitcast(I32))
         load_table(2)
-        nc.sync.dma_start(place[:], offs2)
-        nc.sync.dma_start(out=wgs_sb[:], in_=wgs)
         nc.gpsimd.dma_start(out=gains[:], in_=gain.rearrange("(b p i) -> p b i", b=H_PASSES, i=PACK))
         nc.gpsimd.dma_start(out=bias[:], in_=b1.rearrange("(b p i) -> p b i", b=H_PASSES, i=PACK))
+
+        ident = keep.tile([P, P], F32, name="ident")
+        make_identity(nc, ident[:])
 
         picked = [shared.tile([P, S], U32, name="picked%d" % a, offset=PICKED_AT + a * S * 4) for a in range(K_PASSES)]
 
@@ -108,6 +113,8 @@ def tile_list_crossdock_door_load_kernel(tc, tab_words, tab_scales, offs, w1_wor
         nc.vector.tensor_copy(w1_scales_ordered[:].rearrange("p (b i m) -> p b i m", b=H_PASSES, i=PACK),
                               w1_packed[:].rearrange("p (b m i) -> p b i m", b=H_PASSES, i=PACK))
         w1_planes = unpack_planes(w1_scales_ordered, "w1_planes")
+        nc.sync.dma_start(out=wgs_sb[:], in_=wgs)
+        nc.sync.dma_start(place[:], offs2)
         gather_words(1, 0, S)
         w1_codes = [keep.tile([P, K_PASSES * H], U8, name="w1_codes0", align_bytes=64),
                     shared.tile([P, K_PASSES * H], U8, name="w1_codes1", offset=(K_PASSES - 1) * T * 4)]
@@ -126,8 +133,8 @@ def tile_list_crossdock_door_load_kernel(tc, tab_words, tab_scales, offs, w1_wor
         pages.append(shared.tile([P, T2], F32, name="last_page", offset=0))
         for page in pages:
             nc.gpsimd.memset(page[:], 0.0)
-        z_planes = [keep.tile([P, PACK * T2], BF16, name="z_planes0"),
-                    shared.tile([P, PACK * T2], BF16, name="z_planes1", offset=PLANES_AT)]
+        z_planes = [keep.tile([P, PACK * DIRECT], BF16, name="z_planes0"),
+                    shared.tile([P, PACK * DIRECT], BF16, name="z_planes1", offset=PLANES_AT)]
 
         load_rows = load.rearrange("(b p i) t -> b i p t", b=H_PASSES, i=PACK)
         w2_rows = w2.rearrange("(b p i) n -> b p i n", b=H_PASSES, i=PACK)
@@ -167,7 +174,7 @@ def tile_list_crossdock_door_load_kernel(tc, tab_words, tab_scales, offs, w1_wor
 
         def add_load(engine, r, lo, hi):
             b, i = divmod(r, PACK)
-            engine.tensor_tensor(z_planes[b][:, i * T2 + lo : i * T2 + hi], pages[r % PAGES][:, lo:hi],
+            engine.tensor_tensor(z_planes[b][:, i * DIRECT + lo : i * DIRECT + hi], pages[r % PAGES][:, lo:hi],
                                  held[r][:, lo:hi], ADD)
 
         def copy_on(use_vector, dst, src):
@@ -187,6 +194,42 @@ def tile_list_crossdock_door_load_kernel(tc, tab_words, tab_scales, offs, w1_wor
                             z_grouped[b, q][:, PACK * lo : PACK * hi].rearrange("p (c t i) -> p c i t", i=PACK, t=4),
                             planes[:, :, q * BANK + lo : q * BANK + hi].rearrange("p i (c t) -> p c i t", t=4))
 
+        def turn(acc, region, src, block, start, stop):
+            nc.tensor.matmul(acc[:, region * P : (region + 1) * P], lhsT=src[:, block * P : (block + 1) * P],
+                             rhs=ident[:], start=start, stop=stop, is_transpose=True)
+
+        sums, turned = [], {}
+
+        def add_turned(r):
+            pair, e = divmod(r, 2)
+            if e == 0:
+                sums[:] = [bank(no) for no in SUM_BANKS]
+            for src in (held[r], pages[r % PAGES]):
+                for j, acc in enumerate(sums):
+                    for c in range(2):
+                        turn(acc, 2 * c + e, src, DIRECT // P + 2 * j + c,
+                             src is held[r] and e + c == 0, src is not held[r] and e + c == 2)
+            if e == 1:
+                for j, acc in enumerate(sums):
+                    q, half = divmod(2 * DIRECT_CHUNKS + j, 2)
+                    if half == 0:
+                        turned[pair, q] = ring.tile([P, 2 * BANK], BF16, name="turned", bufs=6)
+                    nc.scalar.copy(
+                        turned[pair, q][:, half * BANK : (half + 1) * BANK].rearrange("t (c p e) -> t c p e", c=2, e=2),
+                        acc[:].rearrange("t (c e p) -> t c p e", c=2, e=2))
+
+        def turn_back(b, q, bank_nos):
+            z_grouped[b, q] = ring.tile([P, PACK * BANK], BF16, name="grouped", bufs=6, align_bytes=64)
+            for half in range(2):
+                acc = bank(bank_nos[half])
+                for u in range(2):
+                    words = turned[2 * b + u, q][:].bitcast(F32)
+                    for c in range(2):
+                        turn(acc, 2 * u + c, words, 2 * half + c, True, True)
+                nc.scalar.copy(
+                    z_grouped[b, q][:].bitcast(F32)[:, half * BANK : (half + 1) * BANK].rearrange("p (t u) -> p t u", u=2),
+                    acc[:].rearrange("p (u t) -> p t u", u=2))
+
         def quantize_z(b, q):
             z_codes[b, q] = keep.tile([P, BANK], U32, name="z_codes%d%d" % (b, q), align_bytes=64)
             z_scales[b, q] = shared.tile([P, BANK], U8, name="z_scales%d%d" % (b, q),
@@ -205,7 +248,8 @@ def tile_list_crossdock_door_load_kernel(tc, tab_words, tab_scales, offs, w1_wor
 
         def second_product(q, bank_nos):
             accs = [bank(no) for no in bank_nos]
-            for b, n in [(b, n) for b in range(H_PASSES) for n in range(N_TILES)]:
+            order = [(b, n) for n in range(N_TILES) for b in range(H_PASSES)]
+            for b, n in sorted(order) if q == 0 else order:
                 cols = slice(b * N + n * P, b * N + (n + 1) * P)
                 nc.tensor.matmul_mx(
                     out=accs[n][:],
@@ -213,8 +257,8 @@ def tile_list_crossdock_door_load_kernel(tc, tab_words, tab_scales, offs, w1_wor
                     rhs=z_codes[b, q][:].bitcast(FP8X4), rhs_scale=z_scales[b, q][:],
                     start=(b == 0), stop=(b == H_PASSES - 1))
             for n in range(N_TILES):
-                result = shared.tile([P, BANK], F32, name="result", bufs=6, offset=PICKED_AT)
-                copy_on(q * N_TILES + n in (11, 13, 15), result[:], accs[n][:])
+                result = shared.tile([P, BANK], F32, name="result", bufs=CHUNKS * N_TILES, offset=ROWS_AT)
+                copy_on((q, n) in ((0, 0), (0, 1), (2, 1), (2, 3), (3, 1), (3, 3)), result[:], accs[n][:])
                 nc.sync.dma_start(out=out[n * P : (n + 1) * P, q * BANK : (q + 1) * BANK], in_=result[:])
 
         for b in range(H_PASSES):
@@ -231,32 +275,36 @@ def tile_list_crossdock_door_load_kernel(tc, tab_words, tab_scales, offs, w1_wor
                 first_product(r + 2)
             if r < last:
                 load_held(r + 1)
-                add_load(nc.gpsimd, r, 0, T2)
+                add_load(nc.gpsimd, r, 0, DIRECT)
+                add_turned(r)
             if r < H_PASSES:
                 round_w2(r)
             if r == last - 1:
                 w2_scales = shared.tile([P, H_PASSES * N], U8, name="w2_scales", offset=H_AT + r % H_SLOTS * S * 4)
                 nc.vector.quantize_mx(out=w2_codes[:].bitcast(FP8X4), scales=w2_scales[:], in_=w2_grouped[:])
             if r == PACK + 1:
-                for q in range(CHUNKS):
+                for q in range(DIRECT_CHUNKS):
                     interleave(0, q, 0)
+                for q in range(DIRECT_CHUNKS, CHUNKS):
+                    turn_back(0, q, (2, 3))
 
         def add_last(q):
             add_load(nc.vector, last, q * BANK, (q + 1) * BANK)
 
         add_last(0)
-        add_last(1)
-        interleave(1, 0, BANK // 2)
         quantize_z(0, 0)
+        interleave(1, 0, BANK // 2)
+        add_turned(last)
+        add_last(1)
         quantize_z(1, 0)
-        interleave(1, 1, 0)
-        add_last(2)
-        add_last(3)
+        interleave(1, 1, BANK)
         quantize_z(0, 1)
         quantize_z(1, 1)
-        for q in range(CHUNKS):
-            if q + 2 < CHUNKS:
-                interleave(1, q + 2, BANK)
-                quantize_z(0, q + 2)
-                quantize_z(1, q + 2)
-            second_product(q, [(q % 2) * N_TILES + n for n in range(N_TILES)])
+        turn_back(1, 2, (4, 5))
+        turn_back(1, 3, (6, 7))
+        second_product(0, (0, 1, 2, 3))
+        for q in range(1, CHUNKS):
+            if q + 1 < CHUNKS:
+                quantize_z(0, q + 1)
+                quantize_z(1, q + 1)
+            second_product(q, [q % 2 * N_TILES + n for n in range(N_TILES)])

@@ -40,6 +40,7 @@ PICKED_AT = K_PASSES * T * 4
 ROWS_AT = PICKED_AT + K_PASSES * S * 4
 H_AT = ROWS_AT + ROW_TILES * T2 * 4
 PLANES_AT = H_AT + H_SLOTS * S * 4
+W1_RAW_AT = PLANES_AT + H_PASSES * PACK * N * 4
 
 
 def tile_list_crossdock_door_load_kernel(tc, tab_words, tab_scales, offs, w1_words, w1_scales, b1, gain, wgs, offs2, load, w2, out):
@@ -59,7 +60,7 @@ def tile_list_crossdock_door_load_kernel(tc, tab_words, tab_scales, offs, w1_wor
         table = [shared.tile([P, T], U32, name="table%d" % a, offset=a * T * 4, align_bytes=64) for a in range(K_PASSES)]
         tab_packed = keep.tile([P, T], U8, name="tab_packed")
         w1_packed = keep.tile([P, H], U8, name="w1_packed")
-        w1_raw = keep.tile([P, K_PASSES * 2 * H], U8, name="w1_raw")
+        w1_raw = shared.tile([P, K_PASSES * 2 * H], U8, name="w1_raw", offset=W1_RAW_AT)
         wgs_sb = keep.tile([P, S], F32, name="wgs_sb")
         bias = keep.tile([P, H_PASSES, PACK], F32, name="bias")
         gains = keep.tile([P, H_PASSES, PACK], F32, name="gains")
@@ -130,10 +131,9 @@ def tile_list_crossdock_door_load_kernel(tc, tab_words, tab_scales, offs, w1_wor
         order_w1_words(1)
 
         pages = [keep.tile([P, T2], F32, name="page%d" % j) for j in range(PAGES - 1)]
-        pages.append(shared.tile([P, T2], F32, name="last_page", offset=0))
         for page in pages:
-            nc.gpsimd.memset(page[:], 0.0)
-        z_planes = [keep.tile([P, PACK * DIRECT], BF16, name="z_planes0"),
+            nc.vector.memset(page[:], 0.0)
+        z_planes = [shared.tile([P, PACK * DIRECT], BF16, name="z_planes0", offset=0),
                     shared.tile([P, PACK * DIRECT], BF16, name="z_planes1", offset=PLANES_AT)]
 
         load_rows = load.rearrange("(b p i) t -> b i p t", b=H_PASSES, i=PACK)
@@ -169,7 +169,8 @@ def tile_list_crossdock_door_load_kernel(tc, tab_words, tab_scales, offs, w1_wor
                 nc.vector.tensor_copy(pages[r % PAGES][:].indirect(place[:, lo // 16 : hi // 16]), h[r][:, lo:hi])
 
         def load_held(r):
-            held[r] = shared.tile([P, T2], F32, name="held%d" % r, offset=ROWS_AT + r * T2 * 4)
+            at = ROWS_AT + r * T2 * 4 if r + 1 < ROW_TILES else W1_RAW_AT
+            held[r] = shared.tile([P, T2], F32, name="held%d" % r, offset=at)
             nc.sync.dma_start(out=held[r][:], in_=load_rows[r // PACK, r % PACK])
 
         def add_load(engine, r, lo, hi):
@@ -265,6 +266,8 @@ def tile_list_crossdock_door_load_kernel(tc, tab_words, tab_scales, offs, w1_wor
             load_w2(b)
         first_product(0)
         first_product(1)
+        pages.append(shared.tile([P, T2], F32, name="last_page", offset=ROWS_AT + (ROW_TILES - 1) * T2 * 4))
+        nc.gpsimd.memset(pages[-1][:], 0.0)
         load_held(0)
         w2_grouped = shared.tile([P, H_PASSES * PACK * N], BF16, name="w2_grouped", offset=T * 4)
         w2_codes = keep.tile([P, H_PASSES * N], U32, name="w2_codes", align_bytes=64)

from contextlib import ExitStack

import concourse.mybir as mybir
from concourse.masks import make_identity

K, H, N, T, S, T2 = 1536, 1024, 512, 2048, 1024, 2048
FLOPS = 2 * K * H * S + 2 * H * N * T2

F32 = mybir.dt.float32
BF16 = mybir.dt.bfloat16
I32 = mybir.dt.int32
U32 = mybir.dt.uint32
U16 = mybir.dt.uint16
U8 = mybir.dt.uint8
FP8X4 = mybir.dt.float8_e4m3fn_x4
FP4X4 = mybir.dt.float4_e2m1fn_x4
MULT = mybir.AluOpType.mult
ADD = mybir.AluOpType.add
TANH = mybir.ActivationFunctionType.Tanh
COPY = mybir.ActivationFunctionType.Copy

P = 128
PACK = 4
BANK = 512
K_PASSES = K // (P * PACK)
H_PASSES = H // (P * PACK)
ROW_TILES = H // P
CHUNKS = T2 // BANK
N_TILES = N // P
QUADRANT = 32
SCALE_ROWS = 4
PACKED_ROWS = K_PASSES * SCALE_ROWS
PLANE_ROWS = 3 * QUADRANT + SCALE_ROWS
PAGES = 3
H_SLOTS = 4
DIRECT_CHUNKS = 2
DIRECT = DIRECT_CHUNKS * BANK
SUM_BANKS = (4, 5, 6, 7)
PICKED_AT = K_PASSES * T * 4
ROWS_AT = PICKED_AT + K_PASSES * S * 4
H_AT = ROWS_AT + ROW_TILES * T2 * 4
PLANES_AT = H_AT + H_SLOTS * S * 4
W1_RAW_AT = PLANES_AT + H_PASSES * PACK * N * 4


def tile_list_crossdock_door_load_kernel(tc, tab_words, tab_scales, offs, w1_words, w1_scales, b1, gain, wgs, offs2, load, w2, out):
    nc = tc.nc
    with ExitStack() as ctx:
        lists = ctx.enter_context(tc.tile_pool(name="lists", bufs=1))
        keep = ctx.enter_context(tc.tile_pool(name="keep", bufs=1))
        shared = ctx.enter_context(tc.tile_pool(name="shared", bufs=1))
        ring = ctx.enter_context(tc.tile_pool(name="ring", bufs=3))
        psum = ctx.enter_context(tc.psum_pool(name="psum", bufs=1))

        def bank(j):
            return psum.tile([P, BANK], F32, name="bank%d" % j)

        pick = lists.tile([P, S // 16], U16, name="pick")
        place = lists.tile([P, S // 16], U16, name="place")
        table = [shared.tile([P, T], U32, name="table%d" % a, offset=a * T * 4, align_bytes=64) for a in range(K_PASSES)]
        tab_packed = keep.tile([P, T], U8, name="tab_packed")
        w1_packed = keep.tile([P, H], U8, name="w1_packed")
        w1_raw = shared.tile([P, K_PASSES * 2 * H], U8, name="w1_raw", offset=W1_RAW_AT)
        wgs_sb = keep.tile([P, S], F32, name="wgs_sb")
        bias = keep.tile([P, H_PASSES, PACK], F32, name="bias")
        gains = keep.tile([P, H_PASSES, PACK], F32, name="gains")

        def load_table(a):
            nc.sync.dma_start(out=table[a][:].bitcast(I32),
                              in_=tab_words[a].rearrange("p t i -> p (t i)").bitcast(I32))

        def load_scale_rows(queues, packed, scales):
            words = packed[:].bitcast(I32)
            nc.vector.memset(words, 0)
            for q, queue in enumerate(queues):
                queue.dma_start(out=words[QUADRANT * q : QUADRANT * q + PACKED_ROWS, :],
                                in_=scales[:, SCALE_ROWS * q : SCALE_ROWS * (q + 1), :].bitcast(I32))

        def unpack_planes(packed, name):
            planes = [packed]
            for a in range(1, K_PASSES):
                plane = keep.tile([P, S], U8, name="%s%d" % (name, a), align_bytes=64)
                nc.vector.memset(plane[3 * QUADRANT :, :].bitcast(I32), 0)
                nc.sync.dma_start(out=plane[:PLANE_ROWS, :].bitcast(I32),
                                    in_=packed[SCALE_ROWS * a : SCALE_ROWS * a + PLANE_ROWS, :].bitcast(I32))
                planes.append(plane)
            return planes

        nc.sync.dma_start(pick[:], offs)
        load_table(0)
        load_scale_rows([nc.scalar] * 4, tab_packed, tab_scales)
        load_scale_rows([nc.sync] * 4, w1_packed, w1_scales)
        load_table(1)
        nc.sync.dma_start(out=w1_raw[:].bitcast(I32).rearrange("p (a c) -> p a c", a=K_PASSES),
                          in_=w1_words.rearrange("a p c -> p a c").bitcast(I32))
        load_table(2)
        nc.gpsimd.dma_start(out=gains[:], in_=gain.rearrange("(b p i) -> p b i", b=H_PASSES, i=PACK))
        nc.gpsimd.dma_start(out=bias[:], in_=b1.rearrange("(b p i) -> p b i", b=H_PASSES, i=PACK))

        ident = keep.tile([P, P], F32, name="ident")
        make_identity(nc, ident[:])

        picked = [shared.tile([P, S], U32, name="picked%d" % a, offset=PICKED_AT + a * S * 4) for a in range(K_PASSES)]

        def gather_words(a, lo, hi):
            nc.vector.tensor_copy(picked[a][:, lo:hi],
                                  table[a][:].indirect(pick[:, lo // 16 : hi // 16]))

        gather_words(0, 0, S)
        picked_scales = keep.tile([P, S], U8, name="picked_scales", align_bytes=64)
        nc.vector.tensor_copy(picked_scales[:], tab_packed[:].indirect(pick[:]))
        tab_planes = unpack_planes(picked_scales, "tab_planes")
        w1_scales_ordered = keep.tile([P, H], U8, name="w1_scales_ordered", align_bytes=64)
        nc.vector.tensor_copy(w1_scales_ordered[:].rearrange("p (b i m) -> p b i m", b=H_PASSES, i=PACK),
                              w1_packed[:].rearrange("p (b m i) -> p b i m", b=H_PASSES, i=PACK))
        w1_planes = unpack_planes(w1_scales_ordered, "w1_planes")
        nc.sync.dma_start(out=wgs_sb[:], in_=wgs)
        nc.sync.dma_start(place[:], offs2)
        gather_words(1, 0, S)
        w1_codes = [keep.tile([P, K_PASSES * H], U8, name="w1_codes0", align_bytes=64),
                    shared.tile([P, K_PASSES * H], U8, name="w1_codes1", offset=(K_PASSES - 1) * T * 4)]

        def order_w1_words(b):
            nc.vector.tensor_copy(
                w1_codes[b][:].bitcast(U16).rearrange("p (a i m) -> p i a m", i=PACK, m=P),
                w1_raw[:].bitcast(U16).rearrange("p (a b m i) -> p b i a m", b=H_PASSES, i=PACK, m=P)[:, b])

        order_w1_words(0)
        gather_words(2, 0, BANK)
        gather_words(2, BANK, S)
        order_w1_words(1)

        pages = [keep.tile([P, T2], F32, name="page%d" % j) for j in range(PAGES - 1)]
        for page in pages:
            nc.vector.memset(page[:], 0.0)
        z_planes = [shared.tile([P, PACK * DIRECT], BF16, name="z_planes0", offset=0),
                    shared.tile([P, PACK * DIRECT], BF16, name="z_planes1", offset=PLANES_AT)]

        load_rows = load.rearrange("(b p i) t -> b i p t", b=H_PASSES, i=PACK)
        w2_rows = w2.rearrange("(b p i) n -> b p i n", b=H_PASSES, i=PACK)
        h, weight, held = {}, {}, {}

        def pieces(r):
            return [(0, 256), (256, 512), (512, S)] if r == 0 else [(0, S)]

        def first_product(r):
            b, i = divmod(r, PACK)
            weight[r] = shared.tile([P, S], F32, name="weight%d" % r, offset=ROWS_AT + (r - 1) % ROW_TILES * T2 * 4)
            nc.scalar.activation(weight[r][:], wgs_sb[:], COPY, scale=gains[:, b, i : i + 1])
            h[r] = shared.tile([P, S], F32, name="h%d" % r, offset=H_AT + r % H_SLOTS * S * 4)
            for half in range(S // BANK):
                cols = slice(half * BANK, (half + 1) * BANK)
                acc = bank(half)
                for a in range(K_PASSES):
                    first = (a * PACK + i) * P
                    nc.tensor.matmul_mx(
                        out=acc[:],
                        lhsT=w1_codes[b][:, 2 * first : 2 * (first + P)].bitcast(FP4X4),
                        lhsT_scale=w1_planes[a][:, r * P : (r + 1) * P],
                        rhs=picked[a][:, cols].bitcast(FP8X4),
                        rhs_scale=tab_planes[a][:, cols],
                        start=(a == 0), stop=(a == K_PASSES - 1))
                nc.scalar.activation(h[r][:, cols], acc[:], TANH, bias=bias[:, b, i : i + 1])
            for lo, hi in pieces(r):
                nc.gpsimd.tensor_tensor(h[r][:, lo:hi], h[r][:, lo:hi], weight[r][:, lo:hi], MULT)

        def scatter(r):
            for lo, hi in pieces(r):
                nc.vector.tensor_copy(pages[r % PAGES][:].indirect(place[:, lo // 16 : hi // 16]), h[r][:, lo:hi])

        def load_held(r):
            at = ROWS_AT + r * T2 * 4 if r + 1 < ROW_TILES else W1_RAW_AT
            held[r] = shared.tile([P, T2], F32, name="held%d" % r, offset=at)
            nc.sync.dma_start(out=held[r][:], in_=load_rows[r // PACK, r % PACK])

        def add_load(engine, r, lo, hi):
            b, i = divmod(r, PACK)
            engine.tensor_tensor(z_planes[b][:, i * DIRECT + lo : i * DIRECT + hi], pages[r % PAGES][:, lo:hi],
                                 held[r][:, lo:hi], ADD)

        def copy_on(use_vector, dst, src):
            if use_vector:
                nc.vector.tensor_copy(dst, src)
            else:
                nc.scalar.copy(dst, src)

        z_grouped, z_codes, z_scales = {}, {}, {}

        def interleave(b, q, vector_cols):
            z_grouped[b, q] = ring.tile([P, PACK * BANK], BF16, name="grouped", bufs=6, align_bytes=64)
            planes = z_planes[b][:].rearrange("p (i t) -> p i t", i=PACK)
            for use_vector, lo, hi in ((False, vector_cols, BANK), (True, 0, vector_cols)):
                if lo < hi:
                    copy_on(use_vector,
                            z_grouped[b, q][:, PACK * lo : PACK * hi].rearrange("p (c t i) -> p c i t", i=PACK, t=4),
                            planes[:, :, q * BANK + lo : q * BANK + hi].rearrange("p i (c t) -> p c i t", t=4))

        def turn(acc, region, src, block, start, stop):
            nc.tensor.matmul(acc[:, region * P : (region + 1) * P], lhsT=src[:, block * P : (block + 1) * P],
                             rhs=ident[:], start=start, stop=stop, is_transpose=True)

        sums, turned = [], {}

        def add_turned(r):
            pair, e = divmod(r, 2)
            if e == 0:
                sums[:] = [bank(no) for no in SUM_BANKS]
            for src in (held[r], pages[r % PAGES]):
                for j, acc in enumerate(sums):
                    for c in range(2):
                        turn(acc, 2 * c + e, src, DIRECT // P + 2 * j + c,
                             src is held[r] and e + c == 0, src is not held[r] and e + c == 2)
            if e == 1:
                for j, acc in enumerate(sums):
                    q, half = divmod(2 * DIRECT_CHUNKS + j, 2)
                    if half == 0:
                        turned[pair, q] = ring.tile([P, 2 * BANK], BF16, name="turned", bufs=6)
                    nc.scalar.copy(
                        turned[pair, q][:, half * BANK : (half + 1) * BANK].rearrange("t (c p e) -> t c p e", c=2, e=2),
                        acc[:].rearrange("t (c e p) -> t c p e", c=2, e=2))

        def turn_back(b, q, bank_nos):
            z_grouped[b, q] = ring.tile([P, PACK * BANK], BF16, name="grouped", bufs=6, align_bytes=64)
            for half in range(2):
                acc = bank(bank_nos[half])
                for u in range(2):
                    words = turned[2 * b + u, q][:].bitcast(F32)
                    for c in range(2):
                        turn(acc, 2 * u + c, words, 2 * half + c, True, True)
                nc.scalar.copy(
                    z_grouped[b, q][:].bitcast(F32)[:, half * BANK : (half + 1) * BANK].rearrange("p (t u) -> p t u", u=2),
                    acc[:].rearrange("p (u t) -> p t u", u=2))

        def quantize_z(b, q):
            z_codes[b, q] = keep.tile([P, BANK], U32, name="z_codes%d%d" % (b, q), align_bytes=64)
            z_scales[b, q] = shared.tile([P, BANK], U8, name="z_scales%d%d" % (b, q),
                                         offset=H_AT + (ROW_TILES - 1) % H_SLOTS * S * 4 + (b * CHUNKS + q) * BANK)
            nc.vector.quantize_mx(out=z_codes[b, q][:].bitcast(FP8X4), scales=z_scales[b, q][:], in_=z_grouped[b, q][:])

        w2_raw = {}

        def load_w2(b):
            w2_raw[b] = shared.tile([P, PACK * N], F32, name="w2_raw%d" % b, offset=PLANES_AT + b * PACK * N * 4)
            nc.sync.dma_start(out=w2_raw[b][:].rearrange("p (i n) -> p i n", i=PACK), in_=w2_rows[b])

        def round_w2(b):
            nc.scalar.copy(w2_grouped[:, b * PACK * N : (b + 1) * PACK * N].rearrange("p (c n i) -> p c i n", i=PACK, n=4),
                           w2_raw[b][:].rearrange("p (i c n) -> p c i n", i=PACK, n=4))

        def second_product(q, bank_nos):
            accs = [bank(no) for no in bank_nos]
            order = [(b, n) for n in range(N_TILES) for b in range(H_PASSES)]
            for b, n in sorted(order) if q == 0 else order:
                cols = slice(b * N + n * P, b * N + (n + 1) * P)
                nc.tensor.matmul_mx(
                    out=accs[n][:],
                    lhsT=w2_codes[:, cols].bitcast(FP8X4), lhsT_scale=w2_scales[:, cols],
                    rhs=z_codes[b, q][:].bitcast(FP8X4), rhs_scale=z_scales[b, q][:],
                    start=(b == 0), stop=(b == H_PASSES - 1))
            for n in range(N_TILES):
                result = shared.tile([P, BANK], F32, name="result", bufs=CHUNKS * N_TILES, offset=ROWS_AT)
                copy_on((q, n) in ((0, 0), (0, 1), (2, 1), (2, 3), (3, 1), (3, 3)), result[:], accs[n][:])
                nc.sync.dma_start(out=out[n * P : (n + 1) * P, q * BANK : (q + 1) * BANK], in_=result[:])

        for b in range(H_PASSES):
            load_w2(b)
        first_product(0)
        first_product(1)
        pages.append(shared.tile([P, T2], F32, name="last_page", offset=ROWS_AT + (ROW_TILES - 1) * T2 * 4))
        nc.gpsimd.memset(pages[-1][:], 0.0)
        load_held(0)
        w2_grouped = shared.tile([P, H_PASSES * PACK * N], BF16, name="w2_grouped", offset=T * 4)
        w2_codes = keep.tile([P, H_PASSES * N], U32, name="w2_codes", align_bytes=64)
        last = ROW_TILES - 1
        for r in range(ROW_TILES):
            scatter(r)
            if r + 2 < ROW_TILES:
                first_product(r + 2)
            if r < last:
                load_held(r + 1)
                add_load(nc.gpsimd, r, 0, DIRECT)
                add_turned(r)
            if r < H_PASSES:
                round_w2(r)
            if r == last - 1:
                w2_scales = shared.tile([P, H_PASSES * N], U8, name="w2_scales", offset=H_AT + r % H_SLOTS * S * 4)
                nc.vector.quantize_mx(out=w2_codes[:].bitcast(FP8X4), scales=w2_scales[:], in_=w2_grouped[:])
            if r == PACK + 1:
                for q in range(DIRECT_CHUNKS):
                    interleave(0, q, 0)
                for q in range(DIRECT_CHUNKS, CHUNKS):
                    turn_back(0, q, (2, 3))

        def add_last(q):
            add_load(nc.vector, last, q * BANK, (q + 1) * BANK)

        add_last(0)
        quantize_z(0, 0)
        interleave(1, 0, BANK // 2)
        add_turned(last)
        add_last(1)
        quantize_z(1, 0)
        interleave(1, 1, BANK)
        quantize_z(0, 1)
        quantize_z(1, 1)
        turn_back(1, 2, (4, 5))
        turn_back(1, 3, (6, 7))
        second_product(0, (0, 1, 2, 3))
        for q in range(1, CHUNKS):
            if q + 1 < CHUNKS:
                quantize_z(0, q + 1)
                quantize_z(1, q + 1)
            second_product(q, [q % 2 * N_TILES + n for n in range(N_TILES)])
